import numpy as np
import ml_dtypes


def mxq(x, axis, fmt="e4m3"):
    dtype, down = {"e4m3": (ml_dtypes.float8_e4m3fn, 7), "e5m2": (ml_dtypes.float8_e5m2, 14)}[fmt]
    v = np.moveaxis(np.asarray(x, np.float32).astype(ml_dtypes.bfloat16).astype(np.float64), axis, -1)
    blocks = v.reshape(v.shape[:-1] + (-1, 32))
    amax = np.abs(blocks).max(-1, keepdims=True)
    byte = np.maximum(np.where(amax > 0, np.frexp(amax)[1] - 1 + 127, 0) - down, 1)
    scale = np.exp2(byte - 127.0)
    codes = (blocks / scale).astype(np.float32).astype(dtype).astype(np.float64)
    return np.moveaxis((codes * scale).reshape(v.shape), -1, axis)


WIDE = False


def mx_kscale(k):
    if not WIDE:
        return np.ones(k)
    levels = np.array([30, -30])
    if k % 512:
        return np.exp2(np.random.permutation(np.resize(levels, k // 32))).repeat(32)
    a = np.empty((k // 512, 16))
    for p in range(k // 512):
        a[p, :8] = np.random.permutation(np.resize(levels, 8))
        for g in range(8):
            far = levels[np.abs(levels - a[p, g]) >= 10]
            a[p, g + 8] = far[np.random.randint(len(far))]
    return np.exp2(a.ravel()).repeat(32)


def f64(x):
    return np.asarray(x).astype(np.float64)


def striped(idx):
    return np.tile(idx.reshape(-1, 16).T, (8, 1)).astype(np.uint16)


def unstriped(offs):
    return offs[:16].T.reshape(-1).astype(np.int64)


E2M1 = np.array([0.0, 0.5, 1.0, 1.5, 2.0, 3.0, 4.0, 6.0, -0.0, -0.5, -1.0, -1.5, -2.0, -3.0, -4.0, -6.0])


def pack_weight(w, fmt):
    k, n = w.shape
    w = f64(np.asarray(w, np.float32).astype(ml_dtypes.bfloat16)).reshape(k // 32, 32, n)
    amax = np.abs(w).max(1)
    if fmt == "e4m3":
        byte = np.frexp(amax)[1] - 1 + 127 - 7
    else:
        mant, ex = np.frexp(amax / 6.0)
        byte = np.where(mant > 0.5, ex, ex - 1) + 127
    byte = np.clip(np.where(amax > 0, byte, 1), 1, 254)
    scaled = (w * np.exp2(127.0 - byte)[:, None, :]).reshape(k, n).astype(np.float32)
    by_word = np.ascontiguousarray(scaled.reshape(k // 512, 128, 4, n).transpose(0, 1, 3, 2))
    if fmt == "e4m3":
        words = by_word.astype(ml_dtypes.float8_e4m3fn).view(np.uint8)
    else:
        c = by_word.astype(ml_dtypes.float4_e2m1fn).view(np.uint8) & 0xF
        words = (c[..., 0::2] | (c[..., 1::2] << 4)).reshape(k // 512, 128, 2 * n)
    return np.ascontiguousarray(words), np.ascontiguousarray(byte.astype(np.uint8).reshape(k // 512, 16, n))


def unpack_weight(words, scales, fmt):
    g, _, n = scales.shape
    words = np.ascontiguousarray(words).reshape(g, 128, n, -1)
    if fmt == "e4m3":
        vals = words.view(ml_dtypes.float8_e4m3fn).astype(np.float64)
    else:
        nib = np.empty((g, 128, n, 4), np.uint8)
        nib[..., 0::2] = words & 0xF
        nib[..., 1::2] = words >> 4
        vals = E2M1[nib]
    vals = vals * np.repeat(np.exp2(scales.astype(np.float64) - 127.0), 8, axis=1)[..., None]
    return vals.transpose(0, 1, 3, 2).reshape(g * 512, n)


def d_relu2(v):
    return 2.0 * np.maximum(v, 0.0)


K, T, E, C, H, N = 384, 1280, 2, 512, 512, 512


def by_expert(wq, xq):
    return np.concatenate([wq[e].T @ xq[:, e * C:(e + 1) * C] for e in range(E)], axis=1)


def setup_inputs():
    n = np.random.standard_normal
    s = mx_kscale(N)[:, None]
    u = mx_kscale(H)
    w2 = [pack_weight(m, "e2m1") for m in n((E, N, H)) / np.sqrt(N) / s[None] * u[None, None, :]]
    w1 = [pack_weight(m, "e2m1") for m in n((E, H, K)) / np.sqrt(H) / u[None, :, None]]
    return {
        "dyT": (n((N, T)) * s).astype(np.float32),
        "a": n((H, E * C)).astype(np.float32),
        "w2_words": np.stack([m[0] for m in w2]),
        "w2_scales": np.stack([m[1] for m in w2]),
        "w1_words": np.stack([m[0] for m in w1]),
        "w1_scales": np.stack([m[1] for m in w1]),
        "gate": np.tile(np.random.uniform(0.2, 1.0, E * C), (N, 1)).astype(np.float32),
        "offs": striped(np.random.permutation(T)[:E * C]),
    }


def reference(dyT, a, w2_words, w2_scales, w1_words, w1_scales, gate, offs):
    idx = unstriped(offs)
    w2 = np.stack([unpack_weight(w2_words[e], w2_scales[e], "e2m1") for e in range(E)])
    w1 = np.stack([unpack_weight(w1_words[e], w1_scales[e], "e2m1") for e in range(E)])
    gq = mxq(f64(gate) * f64(dyT)[:, idx], 0, "e5m2")
    dh = by_expert(w2, gq)
    da = dh * d_relu2(f64(a))
    dx = by_expert(w1, mxq(da, 0, "e5m2"))
    out = np.zeros((K, T))
    out[:, idx] = dx
    return out

from contextlib import ExitStack

import concourse.mybir as mybir

K, T, E, C, H, N = 384, 1280, 2, 512, 512, 512
S = E * C
FLOPS = 2 * S * (N * H + H * K)
BYTES = 4 * (N * T + H * S + S + K * T) + E * (N * H + H * K) * 17 // 32 + 128 * (S // 16) * 2

F32 = mybir.dt.float32
BF16 = mybir.dt.bfloat16
I32 = mybir.dt.int32
U32 = mybir.dt.uint32
U16 = mybir.dt.uint16
U8 = mybir.dt.uint8
FP4X4 = mybir.dt.float4_e2m1fn_x4
E5M2X4 = mybir.dt.float8_e5m2_x4
mult = mybir.AluOpType.mult
maximum = mybir.AluOpType.max
Copy = mybir.ActivationFunctionType.Copy
Relu = mybir.ActivationFunctionType.Relu

P = 128
PACK = 4
KT = K // P


def tile_moe_bdx_mlp_relu2_kernel(
    tc, dyT, a, w2_words, w2_scales, w1_words, w1_scales, gate, offs, out
):
    nc = tc.nc
    with ExitStack() as ctx:
        keep = ctx.enter_context(tc.tile_pool(name="keep", bufs=1))
        psum = ctx.enter_context(tc.psum_pool(name="psum", bufs=1))

        offsets = keep.tile([P, S // 16], U16, name="offsets")
        nc.sync.dma_start(offsets[:], offs)

        sc2_raw = keep.tile([P, E * H], U8, name="sc2_raw", align_bytes=64)
        sc1 = keep.tile([P, E * K], U8, name="sc1", align_bytes=64)
        nc.vector.memset(sc2_raw[:].bitcast(I32), 0)
        nc.vector.memset(sc1[:].bitcast(I32), 0)

        def load_scales(plane, src):
            rows = src.bitcast(I32).rearrange("e s (q r) i -> r (s q) e i", r=4)
            for r in range(4):
                nc.sync.dma_start(
                    plane[r:P:32, :].bitcast(I32).rearrange("p (e i) -> p e i", e=E), rows[r]
                )

        planes = [keep.tile([P, T], F32, name=f"dy{t}") for t in range(PACK)]
        dy_rows = dyT.rearrange("(p t) s -> t p s", t=PACK)
        gates = [keep.tile([P, C], F32, name=f"gate{e}") for e in range(E)]
        a_sb = [keep.tile([P, PACK, C], F32, name=f"a{e}") for e in range(E)]
        a_rows = a.rearrange("(p t) s -> p t s", t=PACK)
        w2_raw = keep.tile([P, E * 2 * H], U8, name="w2_raw", align_bytes=64)
        w1 = keep.tile([P, E * 2 * K], U8, name="w1", align_bytes=64)

        def load_words(dst, src):
            nc.sync.dma_start(
                dst[:].bitcast(I32).rearrange("p (e b) -> p e b", e=E),
                src.bitcast(I32).rearrange("e s p b -> (s p) e b"),
            )

        nc.sync.dma_start(planes[0][:], dy_rows[0])
        nc.sync.dma_start(gates[0][:], gate[0:P, 0:C])
        for t in range(1, PACK):
            nc.sync.dma_start(planes[t][:], dy_rows[t])
        load_words(w2_raw, w2_words)
        load_scales(sc2_raw, w2_scales)
        nc.sync.dma_start(gates[1][:], gate[0:P, C:S])
        nc.sync.dma_start(a_sb[0][:], a_rows[:, :, 0:C])
        load_scales(sc1, w1_scales)
        load_words(w1, w1_words)
        nc.sync.dma_start(a_sb[1][:], a_rows[:, :, C:S])

        results = [keep.tile([P, T], F32, name=f"res{k}") for k in range(KT)]
        for k in range(KT):
            nc.gpsimd.memset(results[k][:], 0.0)

        w2 = keep.tile([P, E * 2 * H], U8, name="w2", align_bytes=64)
        sc2 = keep.tile([P, E * H], U8, name="sc2", align_bytes=64)

        def permute(dst, src):
            nc.vector.tensor_copy(
                out=dst.rearrange("p (e t m) -> p e t m", e=E, t=PACK),
                in_=src.rearrange("p (e m t) -> p e t m", e=E, t=PACK),
            )

        HALF = C // 2

        def interleaved(src, cols):
            return src[:, :, cols].rearrange("p t (c i) -> p c t i", i=4)

        def grouped_view(dst, cols):
            return dst[:, PACK * cols.start : PACK * cols.stop].rearrange("p (c i t) -> p c t i", i=4, t=PACK)

        def quantize(codes, scales, grouped, cols):
            nc.vector.quantize_mx(
                out=codes[:, cols].bitcast(E5M2X4),
                scales=scales[:, cols],
                in_=grouped[:, PACK * cols.start : PACK * cols.stop],
            )

        def mx(bank, words, wplane, col, codes, scales):
            nc.tensor.matmul_mx(
                out=bank[:],
                lhsT=words[:, 2 * col : 2 * (col + P)].bitcast(FP4X4),
                lhsT_scale=wplane[:, col : col + P],
                rhs=codes[:].bitcast(E5M2X4),
                rhs_scale=scales[:],
                start=True,
                stop=True,
            )

        halves = (slice(0, HALF), slice(HALF, C))
        moved = []
        for e in range(E):
            slot_offs = offsets[:, e * (C // 16) : (e + 1) * (C // 16)]
            g = keep.tile([P, PACK, C], F32, name=f"g{e}")
            for t in range(PACK):
                for cols in halves if t == PACK - 1 else (slice(0, C),):
                    nc.vector.tensor_tensor(
                        out=g[:, t, cols],
                        in0=planes[t][:].indirect(offsets[:, (e * C + cols.start) // 16 : (e * C + cols.stop) // 16]),
                        in1=gates[e][:, cols],
                        op=mult,
                    )
            if e == 0:
                permute(w2[:].bitcast(U16), w2_raw[:].bitcast(U16))
                permute(sc2[:], sc2_raw[:])
            else:
                slopes = keep.tile([P, PACK, C], F32, name="slopes")
                nc.scalar.activation(out=slopes[:], in_=a_sb[e][:], func=Relu, scale=2.0)

            g_bf = keep.tile([P, PACK * C], BF16, name=f"g_bf{e}", align_bytes=64)
            g_codes = keep.tile([P, C], U32, name=f"g_codes{e}", align_bytes=64)
            g_scales = keep.tile([P, C], U8, name=f"g_scales{e}", align_bytes=64)
            for cols in halves:
                nc.scalar.activation(out=grouped_view(g_bf, cols), in_=interleaved(g, cols), func=Copy)
                quantize(g_codes, g_scales, g_bf, cols)

            banks = []
            for t in range(PACK):
                dh = psum.tile([P, C], F32, name=f"dh{t}")
                mx(dh, w2, sc2, e * H + t * P, g_codes, g_scales)
                banks.append(dh)
            da = keep.tile([P, PACK, C], F32, name=f"da{e}")
            da_bf = keep.tile([P, PACK * C], BF16, name=f"da_bf{e}", align_bytes=64)
            da_codes = keep.tile([P, C], U32, name=f"da_codes{e}", align_bytes=64)
            da_scales = keep.tile([P, C], U8, name=f"da_scales{e}", align_bytes=64)
            for cols in halves:
                for t in range(PACK):
                    if e == 0:
                        nc.vector.scalar_tensor_tensor(
                            out=da[:, t, cols], in0=a_sb[e][:, t, cols], scalar=0.0, in1=banks[t][:, cols],
                            op0=maximum, op1=mult,
                        )
                    else:
                        nc.scalar.copy(out=da[:, t, cols], in_=banks[t][:, cols])
                if e == 0:
                    nc.scalar.activation(out=grouped_view(da_bf, cols), in_=interleaved(da, cols), func=Copy, scale=2.0)
                else:
                    nc.gpsimd.tensor_tensor(
                        out=grouped_view(da_bf, cols), in0=interleaved(da, cols), in1=interleaved(slopes, cols), op=mult
                    )
                quantize(da_codes, da_scales, da_bf, cols)
            for k in range(KT):
                dx = psum.tile([P, C], F32, name=f"dx{k}")
                mx(dx, w1, sc1, e * K + k * P, da_codes, da_scales)
                dx_sb = keep.tile([P, C], F32, name=f"dxs{e}_{k}")
                nc.scalar.copy(out=dx_sb[:], in_=dx[:])
                moved.append((k, slot_offs, dx_sb))
        for k, slot_offs, dx_sb in moved:
            nc.vector.tensor_copy(out=results[k][:].indirect(slot_offs), in_=dx_sb[:])
        for k in range(KT):
            nc.sync.dma_start(out[k * P : (k + 1) * P, :], results[k][:])
